import numpy as np
import ml_dtypes


def mxq(x, axis, fmt="e4m3"):
    dtype, down = {"e4m3": (ml_dtypes.float8_e4m3fn, 7), "e5m2": (ml_dtypes.float8_e5m2, 14)}[fmt]
    v = np.moveaxis(np.asarray(x, np.float32).astype(ml_dtypes.bfloat16).astype(np.float64), axis, -1)
    blocks = v.reshape(v.shape[:-1] + (-1, 32))
    amax = np.abs(blocks).max(-1, keepdims=True)
    byte = np.maximum(np.where(amax > 0, np.frexp(amax)[1] - 1 + 127, 0) - down, 1)
    scale = np.exp2(byte - 127.0)
    codes = (blocks / scale).astype(np.float32).astype(dtype).astype(np.float64)
    return np.moveaxis((codes * scale).reshape(v.shape), -1, axis)


WIDE = False


def mx_kscale(k):
    if not WIDE:
        return np.ones(k)
    levels = np.array([10, -10, 5, -5, 0])
    if k % 512:
        return np.exp2(np.random.permutation(np.resize(levels, k // 32))).repeat(32)
    a = np.empty((k // 512, 16))
    for p in range(k // 512):
        a[p, :8] = np.random.permutation(np.resize(levels, 8))
        for g in range(8):
            far = levels[np.abs(levels - a[p, g]) >= 10]
            a[p, g + 8] = far[np.random.randint(len(far))]
    return np.exp2(a.ravel()).repeat(32)


def f64(x):
    return np.asarray(x).astype(np.float64)


def striped(idx):
    return np.tile(idx.reshape(-1, 16).T, (8, 1)).astype(np.uint16)


def unstriped(offs):
    return offs[:16].T.reshape(-1).astype(np.int64)


def pack_weight(w):
    k, n = w.shape
    w = f64(np.asarray(w, np.float32).astype(ml_dtypes.bfloat16)).reshape(k // 32, 32, n)
    amax = np.abs(w).max(1)
    byte = np.clip(np.where(amax > 0, np.frexp(amax)[1] - 1 + 127 - 7, 1), 1, 254)
    scaled = (w * np.exp2(127.0 - byte)[:, None, :]).reshape(k, n).astype(np.float32)
    words = np.ascontiguousarray(scaled.reshape(k // 512, 128, 4, n).transpose(0, 1, 3, 2)).astype(ml_dtypes.float8_e4m3fn).view(np.uint8)
    return words, np.ascontiguousarray(byte.astype(np.uint8).reshape(k // 512, 16, n))


def unpack_weight(words, scales):
    g, p, n, _ = words.shape
    vals = np.ascontiguousarray(words).view(ml_dtypes.float8_e4m3fn).astype(np.float64) * np.repeat(np.exp2(scales.astype(np.float64) - 127.0), 8, axis=1)[..., None]
    return vals.transpose(0, 1, 3, 2).reshape(g * 512, n)


K, T, S, N = 1024, 2048, 512, 256
P = 2 ** 7


def setup_inputs():
    n = np.random.standard_normal
    s = mx_kscale(K)[:, None]
    packed_xT = pack_weight(n((K, T)) * s)
    return {
        "x_words": packed_xT[0],
        "x_scales": packed_xT[1],
        "w1": (n((K, N)) / np.sqrt(K) / s).astype(np.float32),
        "w2": (n((K, N)) / np.sqrt(K) / s).astype(np.float32),
        "w3": (n((K, N)) / np.sqrt(K) / s).astype(np.float32),
        "envl": (np.tile(np.random.uniform(0.0, 1.2, T), (P, 1))).astype(np.float32),
        "inv": (np.random.uniform(0.3, 0.8, (N, 1))).astype(np.float32),
        "one": (np.tile(np.random.uniform(0.9, 1.0, S), (P, 1))).astype(np.float32),
        "offs": striped(np.random.permutation(T)[:S]),
        "lag": striped(np.random.permutation(T)[:S]),
    }


def reference(x_words, x_scales, w1, w2, w3, envl, inv, one, offs, lag):
    xq = unpack_weight(x_words, x_scales)[:, unstriped(offs)]
    y0 = mxq(f64(w1), 0, "e4m3").T @ xq
    y1 = mxq(f64(w2), 0, "e4m3").T @ xq
    x_lag = unpack_weight(x_words, x_scales)[:, unstriped(lag)]
    y2 = mxq(f64(w3), 0, "e4m3").T @ x_lag
    y = y0 + y1 * ((f64(envl)[:1][:, unstriped(offs)]) ** 2) + y2 * (f64(envl)[:1][:, unstriped(lag)] + 0.5 * ((f64(envl)[:1][:, unstriped(offs)]) ** 2))
    return y / (np.maximum(f64(inv) * np.abs(y), f64(one)[:1]))

@@ -1,0 +1,244 @@
+from contextlib import ExitStack
+
+import concourse.mybir as mybir
+from concourse.masks import make_identity
+
+K, T, S, N = 1024, 2048, 512, 256
+FLOPS = 3 * 2 * K * S * N
+
+F32 = mybir.dt.float32
+BF16 = mybir.dt.bfloat16
+I32 = mybir.dt.int32
+U32 = mybir.dt.uint32
+U16 = mybir.dt.uint16
+U8 = mybir.dt.uint8
+FP8X4 = mybir.dt.float8_e4m3fn_x4
+ALU = mybir.AluOpType
+ACT = mybir.ActivationFunctionType
+
+P = 128
+PACK = 4
+PASSES = K // (P * PACK)
+JT = S // P
+MT = N // P
+HALF = S // 2
+FLOOR = 2.0 ** -64
+TAGS = {"word_win0": "rows", "raw01": "raw00", "raw11": "raw10", "word_win1": "raw20", "raw21": "env1", "codes00": "scale_win", "codes10": "env_win", "xw110": "env1", "xw111": "grp21"}
+
+
+def tile_picked_ymempol_crest_p_kernel(tc, x_words, x_scales, w1, w2, w3, envl, inv, one, offs, lag, out):
+    nc = tc.nc
+    with ExitStack() as ctx:
+        keep = ctx.enter_context(tc.tile_pool(name="keep", bufs=1))
+        psum = ctx.enter_context(tc.psum_pool(name="psum", bufs=1))
+
+        def sbuf(shape, dtype, name):
+            return keep.tile(shape, dtype, name=name, tag=TAGS.get(name, name), align_bytes=64)
+
+        offs_t = keep.tile([P, S // 16], U16, name="offs_t")
+        lag_t = keep.tile([P, S // 16], U16, name="lag_t")
+        nc.sync.dma_start(offs_t[:], offs)
+        nc.sync.dma_start(lag_t[:], lag)
+        lists = [offs_t, lag_t]
+
+        scale_win = sbuf([P, T], U8, "scale_win")
+        env_win = sbuf([P, T], F32, "env_win")
+        rows = sbuf([P, P], F32, "rows")
+        ident = sbuf([P, P], F32, "ident")
+        nc.sync.dma_start(rows[0:64, :], one.rearrange("r (t p) -> (r t) p", p=P)[0:64, :])
+        nc.sync.dma_start(rows[64:P, :], inv.rearrange("(t p) o -> t (p o)", p=P).partition_broadcast(32))
+        nc.vector.memset(scale_win[:].bitcast(I32), 0)
+        nc.vector.memset(env_win[:], 0.0)
+        make_identity(nc, ident[:])
+        for q in range(4):
+            nc.scalar.dma_start(scale_win[32 * q:32 * q + 8, :].bitcast(I32), x_scales[:, 4 * q:4 * q + 4, :].bitcast(I32))
+        nc.scalar.dma_start(env_win[0:1, :], envl[0:1, :])
+
+        weights = [w1, w2, w3]
+        raw = {}
+        word_win = {}
+        codes = {}
+        planes = {}
+        grouped = {}
+        xs = {}
+        xw = {}
+        env = {}
+        banks = {}
+        terms = {}
+        sums = {}
+
+        def load_w(i, g):
+            raw[i, g] = sbuf([P, PACK, N], F32, "raw%d%d" % (i, g))
+            nc.sync.dma_start(raw[i, g][:], weights[i][g * 512:(g + 1) * 512, :].rearrange("(p t) m -> p t m", t=PACK))
+
+        def load_x(g):
+            word_win[g] = sbuf([P, T], I32, "word_win%d" % g)
+            nc.sync.dma_start(word_win[g][:], x_words[g].rearrange("p n t -> p (n t)").bitcast(I32))
+
+        def cast_w(i, g, eng):
+            grouped[i, g] = sbuf([P, N, PACK], BF16, "grp%d%d" % (i, g))
+            dst = grouped[i, g][:].rearrange("p (c n) t -> p c t n", n=4)
+            src = raw[i, g][:].rearrange("p t (c n) -> p c t n", n=4)
+            if eng == "s":
+                nc.scalar.copy(dst, src)
+            elif eng == "g":
+                nc.gpsimd.tensor_scalar(dst, src, 1.0, 0.0, ALU.mult, ALU.add)
+            else:
+                nc.vector.tensor_copy(dst, src)
+
+        def quant_w(i, g):
+            codes[i, g] = sbuf([P, N], U32, "codes%d%d" % (i, g))
+            planes[i, g] = sbuf([P, N], U8, "plane%d%d" % (i, g))
+            nc.vector.quantize_mx(out=codes[i, g][:].bitcast(FP8X4), scales=planes[i, g][:], in_=grouped[i, g][:].rearrange("p m t -> p (m t)"))
+
+        def gather_scales(l):
+            xs[l] = sbuf([P, S], U8, "xs%d" % l)
+            nc.vector.tensor_copy(xs[l][:], scale_win[:].indirect(lists[l][:]))
+
+        def gather_env(l):
+            env[l] = sbuf([P, S], F32, "env%d" % l)
+            nc.vector.tensor_copy(env[l][:], env_win[:].indirect(lists[l][:]))
+
+        def gather_words(l, g):
+            whole = sbuf([P, S], U32, "xw%d%d" % (l, g))
+            nc.vector.tensor_copy(whole[:], word_win[g][:].bitcast(U32).indirect(lists[l][:]))
+            xw[l, g, 0] = whole[:, 0:HALF]
+            xw[l, g, 1] = whole[:, HALF:S]
+
+        def gather_half(l, g, h):
+            half = sbuf([P, HALF], U32, "xw%d%d%d" % (l, g, h))
+            nc.vector.tensor_copy(half[:], word_win[g][:].bitcast(U32).indirect(lists[l][:, 16 * h:16 * (h + 1)]))
+            xw[l, g, h] = half[:]
+
+        floored = keep.tile([P, 2, JT], F32, name="floored")
+        recip = keep.tile([P, 2, JT], F32, name="recip")
+        neg_limit = keep.tile([P, MT], F32, name="neg_limit")
+        pair = keep.tile([P, JT, 2], F32, name="pair")
+        scaled = keep.tile([P, JT, 2], F32, name="scaled")
+        lag_gain = keep.tile([P, JT], F32, name="lag_gain")
+        gains = [lambda t: recip[:, 0, t:t + 1], lambda t: scaled[:, t, 0:1], lambda t: lag_gain[:, t:t + 1]]
+
+        def small():
+            rows_ps = psum.tile([P, 2, 64], F32, name="rows_ps", tag="y2_1")
+            nc.tensor.transpose(rows_ps[:].rearrange("p a b -> p (a b)"), rows[:], ident[:])
+            nc.vector.tensor_scalar(floored[:], rows_ps[:, :, 0:JT], FLOOR, None, ALU.max)
+
+        def small2():
+            nc.vector.reciprocal(recip[:], floored[:])
+            nc.scalar.activation(neg_limit[:], recip[:, 1, 0:MT], ACT.Copy, scale=-1.0)
+
+        def make_gains():
+            env_ps = []
+            for l in range(2):
+                env_ps.append(psum.tile([P, JT, P], F32, name="env_ps%d" % l, tag="out_%d" % l))
+                for t in range(JT):
+                    nc.tensor.transpose(env_ps[l][:, t, :], env[l][:, t * P:(t + 1) * P], ident[:])
+            nc.scalar.activation(pair[:, :, 0], env_ps[0][:, :, 0], ACT.Square)
+            nc.scalar.activation(pair[:, :, 1], env_ps[1][:, :, 0], ACT.Copy)
+            for t in range(JT):
+                nc.scalar.activation(scaled[:, t, :], pair[:, t, :], ACT.Copy, scale=recip[:, 0, t:t + 1])
+            for t in range(JT):
+                nc.scalar.activation(lag_gain[:, t:t + 1], scaled[:, t, 0:1], ACT.Identity, scale=0.5, bias=scaled[:, t, 1:2])
+
+        def product(i, g, h):
+            l = 0 if i < 2 else 1
+            if g == 0:
+                banks[i, h] = psum.tile([P, 2, N], F32, name="y%d_%d" % (i, h), tag="y%d_%d" % (i, h))
+            for u in range(2):
+                nc.tensor.matmul_mx(
+                    out=banks[i, h][:, u, :],
+                    lhsT=xw[l, g, h][:, u * P:(u + 1) * P].bitcast(FP8X4),
+                    lhsT_scale=xs[l][4 * g:P, (2 * h + u) * P:(2 * h + u + 1) * P],
+                    rhs=codes[i, g][:].bitcast(FP8X4),
+                    rhs_scale=planes[i, g][:],
+                    start=(g == 0 and u == 0),
+                    stop=(g == PASSES - 1 and u == 1),
+                )
+
+        def weigh(i, h, eng, onto=None):
+            for u in range(2):
+                t = 2 * h + u
+                terms[i, t] = sbuf([P, N], F32, "term%d%d" % (i, t))
+                src = banks[i, h][:, u, :]
+                if eng == "s":
+                    nc.scalar.activation(terms[i, t][:], src, ACT.Copy, scale=gains[i](t))
+                elif onto is None:
+                    nc.vector.tensor_scalar(terms[i, t][:], src, gains[i](t), None, ALU.mult)
+                else:
+                    nc.vector.scalar_tensor_tensor(terms[i, t][:], src, gains[i](t), terms[onto, t][:], ALU.mult, ALU.add)
+
+        def turn(i, h):
+            if i == 0:
+                sums[h] = psum.tile([P, MT, HALF], F32, name="sum%d" % h, tag="out_%d" % h)
+            for u in range(2):
+                for mt in range(MT):
+                    nc.tensor.matmul(
+                        sums[h][:, mt, u * P:(u + 1) * P],
+                        terms[i, 2 * h + u][:, mt * P:(mt + 1) * P],
+                        ident[:],
+                        start=(i == 0 and u == 0 and mt == 0),
+                        stop=(i == 2 and u == 1 and mt == MT - 1),
+                        is_transpose=True,
+                    )
+
+        def finish(h):
+            res = sbuf([P, MT, HALF], F32, "res%d" % h)
+            for mt in range(MT):
+                nc.vector.tensor_scalar(res[:, mt, :], sums[h][:, mt, :], recip[:, 1, mt:mt + 1], neg_limit[:, mt:mt + 1], ALU.min, ALU.max)
+            nc.sync.dma_start(out[:, h * HALF:(h + 1) * HALF].rearrange("(mt p) j -> p mt j", p=P), res[:])
+
+        load_w(0, 0)
+        load_w(1, 0)
+        load_w(2, 0)
+        small()
+        load_x(0)
+        gather_scales(0)
+        small2()
+        gather_scales(1)
+        gather_env(0)
+        gather_env(1)
+        cast_w(0, 0, "s")
+        load_w(0, 1)
+        cast_w(1, 0, "s")
+        load_w(1, 1)
+        cast_w(2, 0, "s")
+        load_x(1)
+        make_gains()
+        load_w(2, 1)
+        quant_w(0, 0)
+        quant_w(1, 0)
+        quant_w(2, 0)
+        gather_words(0, 0)
+        gather_words(1, 0)
+        for i in range(3):
+            product(i, 0, 0)
+            product(i, 0, 1)
+        cast_w(0, 1, "s")
+        cast_w(1, 1, "s")
+        quant_w(0, 1)
+        quant_w(1, 1)
+        gather_half(0, 1, 0)
+        gather_half(0, 1, 1)
+        product(0, 1, 0)
+        product(1, 1, 0)
+        product(0, 1, 1)
+        product(1, 1, 1)
+        cast_w(2, 1, "v")
+        gather_half(1, 1, 0)
+        quant_w(2, 1)
+        gather_half(1, 1, 1)
+        weigh(0, 0, "s")
+        weigh(1, 0, "s")
+        weigh(0, 1, "s")
+        weigh(1, 1, "s")
+        product(2, 1, 0)
+        product(2, 1, 1)
+        turn(0, 0)
+        turn(0, 1)
+        turn(1, 1)
+        weigh(2, 0, "v", 1)
+        weigh(2, 1, "s")
+        turn(2, 0)
+        turn(2, 1)
+        finish(0)
+        finish(1)

@@ -1,7 +1,6 @@
 from contextlib import ExitStack
 
 import concourse.mybir as mybir
-from concourse.masks import make_identity
 
 K, T, S, N = 1024, 2048, 512, 256
 FLOPS = 3 * 2 * K * S * N
@@ -23,7 +22,7 @@ JT = S // P
 MT = N // P
 HALF = S // 2
 FLOOR = 2.0 ** -64
-TAGS = {"word_win0": "rows", "raw01": "raw00", "raw11": "raw10", "word_win1": "raw20", "raw21": "env1", "codes00": "scale_win", "codes10": "env_win", "xw110": "env1", "xw111": "grp21"}
+TAGS = {"word_win1": "raw10", "pair": "raw20", "raw11": "grp10", "term0": "grp10", "raw21": "grp20", "xw1": "grp01", "grp21": "grp11", "xw_last": "grp11", "codes11": "codes01"}
 
 
 def tile_picked_ymempol_crest_p_kernel(tc, x_words, x_scales, w1, w2, w3, envl, inv, one, offs, lag, out):
@@ -32,8 +31,12 @@ def tile_picked_ymempol_crest_p_kernel(tc, x_words, x_scales, w1, w2, w3, envl, 
         keep = ctx.enter_context(tc.tile_pool(name="keep", bufs=1))
         psum = ctx.enter_context(tc.psum_pool(name="psum", bufs=1))
 
+        pools = {}
+
         def sbuf(shape, dtype, name):
-            return keep.tile(shape, dtype, name=name, tag=TAGS.get(name, name), align_bytes=64)
+            tag = TAGS.get(name, name)
+            pool = pools["stage"] if tag != "raw00" and tag.startswith(("raw", "word_win", "one_rows", "inv_t")) else keep
+            return pool.tile(shape, dtype, name=name, tag=tag, align_bytes=64)
 
         offs_t = keep.tile([P, S // 16], U16, name="offs_t")
         lag_t = keep.tile([P, S // 16], U16, name="lag_t")
@@ -42,17 +45,25 @@ def tile_picked_ymempol_crest_p_kernel(tc, x_words, x_scales, w1, w2, w3, envl, 
         lists = [offs_t, lag_t]
 
         scale_win = sbuf([P, T], U8, "scale_win")
-        env_win = sbuf([P, T], F32, "env_win")
-        rows = sbuf([P, P], F32, "rows")
         ident = sbuf([P, P], F32, "ident")
-        nc.sync.dma_start(rows[0:64, :], one.rearrange("r (t p) -> (r t) p", p=P)[0:64, :])
-        nc.sync.dma_start(rows[64:P, :], inv.rearrange("(t p) o -> t (p o)", p=P).partition_broadcast(32))
-        nc.vector.memset(scale_win[:].bitcast(I32), 0)
-        nc.vector.memset(env_win[:], 0.0)
-        make_identity(nc, ident[:])
+        env_win = sbuf([P, T], F32, "env_win")
+        with tc.tile_pool(name="head", bufs=1) as head:
+            zeros = head.tile([P, P], F32, name="zeros", align_bytes=64)
+            nc.sync.dma_start(env_win[96:P, :], envl[0:32, :])
+            nc.vector.memset(scale_win[:].bitcast(I32), 0)
+            nc.vector.memset(zeros[:], 0.0)
+            nc.vector.memset(env_win[0:96, :], 0.0)
+            nc.gpsimd.affine_select(out=ident[:], in_=zeros[:], compare_op=ALU.not_equal, fill=1.0, base=0, pattern=[[-1, P]], channel_multiplier=1)
         for q in range(4):
-            nc.scalar.dma_start(scale_win[32 * q:32 * q + 8, :].bitcast(I32), x_scales[:, 4 * q:4 * q + 4, :].bitcast(I32))
-        nc.scalar.dma_start(env_win[0:1, :], envl[0:1, :])
+            (nc.scalar if q % 2 else nc.sync).dma_start(scale_win[32 * q:32 * q + 8, :].bitcast(I32), x_scales[:, 4 * q:4 * q + 4, :].bitcast(I32))
+        pools["stage"] = ctx.enter_context(tc.tile_pool(name="stage", bufs=1))
+        held = {}
+
+        def load_one():
+            one_rows = sbuf([P, P], F32, "one_rows")
+            nc.sync.dma_start(one_rows[:], one.rearrange("r (t p) -> (r t) p", p=P)[0:P, :])
+            held["one_ps"] = psum.tile([P, P], F32, name="one_ps", tag="y2_1")
+            nc.tensor.transpose(held["one_ps"][:], one_rows[:], ident[:])
 
         weights = [w1, w2, w3]
         raw = {}
@@ -80,7 +91,7 @@ def tile_picked_ymempol_crest_p_kernel(tc, x_words, x_scales, w1, w2, w3, envl, 
             dst = grouped[i, g][:].rearrange("p (c n) t -> p c t n", n=4)
             src = raw[i, g][:].rearrange("p t (c n) -> p c t n", n=4)
             if eng == "s":
-                nc.scalar.copy(dst, src)
+                nc.scalar.activation(dst, src, ACT.Copy)
             elif eng == "g":
                 nc.gpsimd.tensor_scalar(dst, src, 1.0, 0.0, ALU.mult, ALU.add)
             else:
@@ -106,37 +117,51 @@ def tile_picked_ymempol_crest_p_kernel(tc, x_words, x_scales, w1, w2, w3, envl, 
             xw[l, g, 1] = whole[:, HALF:S]
 
         def gather_half(l, g, h):
-            half = sbuf([P, HALF], U32, "xw%d%d%d" % (l, g, h))
-            nc.vector.tensor_copy(half[:], word_win[g][:].bitcast(U32).indirect(lists[l][:, 16 * h:16 * (h + 1)]))
-            xw[l, g, h] = half[:]
+            if (l, h) == (1, 1):
+                half = sbuf([P, HALF], U32, "xw_last")[:]
+            else:
+                if g not in held:
+                    held[g] = sbuf([P, 3 * HALF], U32, "xw%d" % g)
+                half = held[g][:, l * S + h * HALF:l * S + (h + 1) * HALF]
+            nc.vector.tensor_copy(half, word_win[g][:].bitcast(U32).indirect(lists[l][:, 16 * h:16 * (h + 1)]))
+            xw[l, g, h] = half
 
-        floored = keep.tile([P, 2, JT], F32, name="floored")
-        recip = keep.tile([P, 2, JT], F32, name="recip")
-        neg_limit = keep.tile([P, MT], F32, name="neg_limit")
-        pair = keep.tile([P, JT, 2], F32, name="pair")
+        recip = keep.tile([P, JT + 2 * MT], F32, name="recip")
         scaled = keep.tile([P, JT, 2], F32, name="scaled")
         lag_gain = keep.tile([P, JT], F32, name="lag_gain")
-        gains = [lambda t: recip[:, 0, t:t + 1], lambda t: scaled[:, t, 0:1], lambda t: lag_gain[:, t:t + 1]]
+        gains = [lambda t: recip[:, t:t + 1], lambda t: scaled[:, t, 0:1], lambda t: lag_gain[:, t:t + 1]]
+
+        def load_env():
+            nc.sync.dma_start(env_win[0:1, :], envl[0:1, :])
 
         def small():
-            rows_ps = psum.tile([P, 2, 64], F32, name="rows_ps", tag="y2_1")
-            nc.tensor.transpose(rows_ps[:].rearrange("p a b -> p (a b)"), rows[:], ident[:])
-            nc.vector.tensor_scalar(floored[:], rows_ps[:, :, 0:JT], FLOOR, None, ALU.max)
+            held["pair"] = sbuf([P, 2 * JT + JT + MT], F32, "pair")
+            positive = held["pair"][:, 2 * JT:3 * JT + MT]
+            held["floored"] = floored = sbuf([P, JT + 2 * MT], F32, "floored")
+            nc.scalar.activation(positive[:, 0:JT], held["one_ps"][:, 0:JT], ACT.Relu)
+            nc.scalar.activation(positive[:, JT:JT + MT], held["inv_t"][:], ACT.Relu)
+            nc.scalar.activation(floored[:, 0:JT + MT], positive, ACT.Copy, bias=FLOOR)
+            nc.scalar.activation(floored[:, JT + MT:JT + 2 * MT], positive[:, JT:JT + MT], ACT.Copy, scale=-1.0, bias=-FLOOR)
 
         def small2():
-            nc.vector.reciprocal(recip[:], floored[:])
-            nc.scalar.activation(neg_limit[:], recip[:, 1, 0:MT], ACT.Copy, scale=-1.0)
+            nc.vector.reciprocal(recip[:], held["floored"][:])
+
+        def load_inv():
+            held["inv_t"] = inv_t = sbuf([P, MT], F32, "inv_t")
+            with nc.allow_non_contiguous_dma(reason="one value a partition"):
+                nc.sync.dma_start(inv_t[:], inv.rearrange("(t p) o -> p (t o)", p=P))
 
         def make_gains():
             env_ps = []
+            pair = held["pair"][:, 0:2 * JT].rearrange("p (t e) -> p t e", e=2)
             for l in range(2):
                 env_ps.append(psum.tile([P, JT, P], F32, name="env_ps%d" % l, tag="out_%d" % l))
                 for t in range(JT):
                     nc.tensor.transpose(env_ps[l][:, t, :], env[l][:, t * P:(t + 1) * P], ident[:])
-            nc.scalar.activation(pair[:, :, 0], env_ps[0][:, :, 0], ACT.Square)
-            nc.scalar.activation(pair[:, :, 1], env_ps[1][:, :, 0], ACT.Copy)
+            nc.scalar.activation(pair[:, :, 0], env_ps[0][:, :, 96], ACT.Square)
+            nc.scalar.activation(pair[:, :, 1], env_ps[1][:, :, 96], ACT.Copy)
             for t in range(JT):
-                nc.scalar.activation(scaled[:, t, :], pair[:, t, :], ACT.Copy, scale=recip[:, 0, t:t + 1])
+                nc.scalar.activation(scaled[:, t, :], pair[:, t, :], ACT.Copy, scale=recip[:, t:t + 1])
             for t in range(JT):
                 nc.scalar.activation(lag_gain[:, t:t + 1], scaled[:, t, 0:1], ACT.Identity, scale=0.5, bias=scaled[:, t, 1:2])
 
@@ -158,14 +183,16 @@ def tile_picked_ymempol_crest_p_kernel(tc, x_words, x_scales, w1, w2, w3, envl, 
         def weigh(i, h, eng, onto=None):
             for u in range(2):
                 t = 2 * h + u
-                terms[i, t] = sbuf([P, N], F32, "term%d%d" % (i, t))
+                if t == 0:
+                    held["term", i] = sbuf([P, JT, N], F32, "term%d" % i)
+                terms[i, t] = held["term", i][:, t, :]
                 src = banks[i, h][:, u, :]
                 if eng == "s":
-                    nc.scalar.activation(terms[i, t][:], src, ACT.Copy, scale=gains[i](t))
+                    nc.scalar.activation(terms[i, t], src, ACT.Copy, scale=gains[i](t))
                 elif onto is None:
-                    nc.vector.tensor_scalar(terms[i, t][:], src, gains[i](t), None, ALU.mult)
+                    nc.vector.tensor_scalar(terms[i, t], src, gains[i](t), None, ALU.mult)
                 else:
-                    nc.vector.scalar_tensor_tensor(terms[i, t][:], src, gains[i](t), terms[onto, t][:], ALU.mult, ALU.add)
+                    nc.vector.scalar_tensor_tensor(terms[i, t], src, gains[i](t), terms[onto, t], ALU.mult, ALU.add)
 
         def turn(i, h):
             if i == 0:
@@ -184,59 +211,61 @@ def tile_picked_ymempol_crest_p_kernel(tc, x_words, x_scales, w1, w2, w3, envl, 
         def finish(h):
             res = sbuf([P, MT, HALF], F32, "res%d" % h)
             for mt in range(MT):
-                nc.vector.tensor_scalar(res[:, mt, :], sums[h][:, mt, :], recip[:, 1, mt:mt + 1], neg_limit[:, mt:mt + 1], ALU.min, ALU.max)
+                nc.vector.tensor_scalar(res[:, mt, :], sums[h][:, mt, :], recip[:, JT + mt:JT + mt + 1], recip[:, JT + MT + mt:JT + MT + mt + 1], ALU.min, ALU.max)
             nc.sync.dma_start(out[:, h * HALF:(h + 1) * HALF].rearrange("(mt p) j -> p mt j", p=P), res[:])
 
         load_w(0, 0)
         load_w(1, 0)
+        load_one()
+        load_inv()
         load_w(2, 0)
-        small()
         load_x(0)
+        load_w(0, 1)
         gather_scales(0)
-        small2()
         gather_scales(1)
         gather_env(0)
         gather_env(1)
         cast_w(0, 0, "s")
-        load_w(0, 1)
         cast_w(1, 0, "s")
-        load_w(1, 1)
         cast_w(2, 0, "s")
         load_x(1)
-        make_gains()
-        load_w(2, 1)
+        small()
         quant_w(0, 0)
+        small2()
+        make_gains()
+        load_w(1, 1)
         quant_w(1, 0)
         quant_w(2, 0)
+        load_w(2, 1)
         gather_words(0, 0)
         gather_words(1, 0)
         for i in range(3):
             product(i, 0, 0)
             product(i, 0, 1)
         cast_w(0, 1, "s")
-        cast_w(1, 1, "s")
         quant_w(0, 1)
-        quant_w(1, 1)
         gather_half(0, 1, 0)
         gather_half(0, 1, 1)
         product(0, 1, 0)
-        product(1, 1, 0)
         product(0, 1, 1)
+        gather_half(1, 1, 0)
+        cast_w(1, 1, "s")
+        quant_w(1, 1)
+        product(1, 1, 0)
         product(1, 1, 1)
         cast_w(2, 1, "v")
-        gather_half(1, 1, 0)
         quant_w(2, 1)
         gather_half(1, 1, 1)
         weigh(0, 0, "s")
-        weigh(1, 0, "s")
         weigh(0, 1, "s")
+        weigh(1, 0, "s")
         weigh(1, 1, "s")
         product(2, 1, 0)
         product(2, 1, 1)
         turn(0, 0)
         turn(0, 1)
-        turn(1, 1)
         weigh(2, 0, "v", 1)
+        turn(1, 1)
         weigh(2, 1, "s")
         turn(2, 0)
         turn(2, 1)

@@ -88,9 +88,11 @@ def tile_picked_ymempol_crest_p_kernel(tc, x_words, x_scales, w1, w2, w3, envl, 
 
         def cast_w(i, g, eng):
             grouped[i, g] = sbuf([P, N, PACK], BF16, "grp%d%d" % (i, g))
-            dst = grouped[i, g][:].rearrange("p (c n) t -> p c t n", n=4)
-            src = raw[i, g][:].rearrange("p t (c n) -> p c t n", n=4)
+            dst = grouped[i, g][:].rearrange("p (c n) t -> p c t n", n=2)
+            src = raw[i, g][:].rearrange("p t (c n) -> p c t n", n=2)
             if eng == "s":
+                nc.scalar.copy(dst, src)
+            elif eng == "a":
                 nc.scalar.activation(dst, src, ACT.Copy)
             elif eng == "g":
                 nc.gpsimd.tensor_scalar(dst, src, 1.0, 0.0, ALU.mult, ALU.add)
@@ -212,20 +214,20 @@ def tile_picked_ymempol_crest_p_kernel(tc, x_words, x_scales, w1, w2, w3, envl, 
             res = sbuf([P, MT, HALF], F32, "res%d" % h)
             for mt in range(MT):
                 nc.vector.tensor_scalar(res[:, mt, :], sums[h][:, mt, :], recip[:, JT + mt:JT + mt + 1], recip[:, JT + MT + mt:JT + MT + mt + 1], ALU.min, ALU.max)
-            nc.sync.dma_start(out[:, h * HALF:(h + 1) * HALF].rearrange("(mt p) j -> p mt j", p=P), res[:])
+                (nc.sync if mt else nc.scalar).dma_start(out[mt * P:(mt + 1) * P, h * HALF:(h + 1) * HALF], res[:, mt, :])
 
         load_w(0, 0)
         load_w(1, 0)
+        load_w(2, 0)
         load_one()
         load_inv()
-        load_w(2, 0)
         load_x(0)
         load_w(0, 1)
         gather_scales(0)
         gather_scales(1)
         gather_env(0)
         gather_env(1)
-        cast_w(0, 0, "s")
+        cast_w(0, 0, "a")
         cast_w(1, 0, "s")
         cast_w(2, 0, "s")
         load_x(1)

from contextlib import ExitStack

import concourse.mybir as mybir

K, T, S, N = 1024, 2048, 512, 256
FLOPS = 3 * 2 * K * S * N

F32 = mybir.dt.float32
BF16 = mybir.dt.bfloat16
I32 = mybir.dt.int32
U32 = mybir.dt.uint32
U16 = mybir.dt.uint16
U8 = mybir.dt.uint8
FP8X4 = mybir.dt.float8_e4m3fn_x4
ALU = mybir.AluOpType
ACT = mybir.ActivationFunctionType

P = 128
PACK = 4
PASSES = K // (P * PACK)
JT = S // P
MT = N // P
HALF = S // 2
FLOOR = 2.0 ** -64
TAGS = {"word_win1": "raw10", "pair": "raw20", "raw11": "grp10", "term0": "grp10", "raw21": "grp20", "xw1": "grp01", "grp21": "grp11", "xw_last": "grp11", "codes11": "codes01"}


def tile_picked_ymempol_crest_p_kernel(tc, x_words, x_scales, w1, w2, w3, envl, inv, one, offs, lag, out):
    nc = tc.nc
    with ExitStack() as ctx:
        keep = ctx.enter_context(tc.tile_pool(name="keep", bufs=1))
        psum = ctx.enter_context(tc.psum_pool(name="psum", bufs=1))

        pools = {}

        def sbuf(shape, dtype, name):
            tag = TAGS.get(name, name)
            pool = pools["stage"] if tag != "raw00" and tag.startswith(("raw", "word_win", "one_rows", "inv_t")) else keep
            return pool.tile(shape, dtype, name=name, tag=tag, align_bytes=64)

        offs_t = keep.tile([P, S // 16], U16, name="offs_t")
        lag_t = keep.tile([P, S // 16], U16, name="lag_t")
        nc.sync.dma_start(offs_t[:], offs)
        nc.sync.dma_start(lag_t[:], lag)
        lists = [offs_t, lag_t]

        scale_win = sbuf([P, T], U8, "scale_win")
        ident = sbuf([P, P], F32, "ident")
        env_win = sbuf([P, T], F32, "env_win")
        with tc.tile_pool(name="head", bufs=1) as head:
            zeros = head.tile([P, P], F32, name="zeros", align_bytes=64)
            nc.sync.dma_start(env_win[96:P, :], envl[0:32, :])
            nc.vector.memset(scale_win[:].bitcast(I32), 0)
            nc.vector.memset(zeros[:], 0.0)
            nc.vector.memset(env_win[0:96, :], 0.0)
            nc.gpsimd.affine_select(out=ident[:], in_=zeros[:], compare_op=ALU.not_equal, fill=1.0, base=0, pattern=[[-1, P]], channel_multiplier=1)
        for q in range(4):
            (nc.scalar if q % 2 else nc.sync).dma_start(scale_win[32 * q:32 * q + 8, :].bitcast(I32), x_scales[:, 4 * q:4 * q + 4, :].bitcast(I32))
        pools["stage"] = ctx.enter_context(tc.tile_pool(name="stage", bufs=1))
        held = {}

        def load_one():
            one_rows = sbuf([P, P], F32, "one_rows")
            nc.sync.dma_start(one_rows[:], one.rearrange("r (t p) -> (r t) p", p=P)[0:P, :])
            held["one_ps"] = psum.tile([P, P], F32, name="one_ps", tag="y2_1")
            nc.tensor.transpose(held["one_ps"][:], one_rows[:], ident[:])

        weights = [w1, w2, w3]
        raw = {}
        word_win = {}
        codes = {}
        planes = {}
        grouped = {}
        xs = {}
        xw = {}
        env = {}
        banks = {}
        terms = {}
        sums = {}

        def load_w(i, g):
            raw[i, g] = sbuf([P, PACK, N], F32, "raw%d%d" % (i, g))
            nc.sync.dma_start(raw[i, g][:], weights[i][g * 512:(g + 1) * 512, :].rearrange("(p t) m -> p t m", t=PACK))

        def load_x(g):
            word_win[g] = sbuf([P, T], I32, "word_win%d" % g)
            nc.sync.dma_start(word_win[g][:], x_words[g].rearrange("p n t -> p (n t)").bitcast(I32))

        def cast_w(i, g, eng):
            grouped[i, g] = sbuf([P, N, PACK], BF16, "grp%d%d" % (i, g))
            dst = grouped[i, g][:].rearrange("p (c n) t -> p c t n", n=2)
            src = raw[i, g][:].rearrange("p t (c n) -> p c t n", n=2)
            if eng == "s":
                nc.scalar.copy(dst, src)
            elif eng == "a":
                nc.scalar.activation(dst, src, ACT.Copy)
            elif eng == "g":
                nc.gpsimd.tensor_scalar(dst, src, 1.0, 0.0, ALU.mult, ALU.add)
            else:
                nc.vector.tensor_copy(dst, src)

        def quant_w(i, g):
            codes[i, g] = sbuf([P, N], U32, "codes%d%d" % (i, g))
            planes[i, g] = sbuf([P, N], U8, "plane%d%d" % (i, g))
            nc.vector.quantize_mx(out=codes[i, g][:].bitcast(FP8X4), scales=planes[i, g][:], in_=grouped[i, g][:].rearrange("p m t -> p (m t)"))

        def gather_scales(l):
            xs[l] = sbuf([P, S], U8, "xs%d" % l)
            nc.vector.tensor_copy(xs[l][:], scale_win[:].indirect(lists[l][:]))

        def gather_env(l):
            env[l] = sbuf([P, S], F32, "env%d" % l)
            nc.vector.tensor_copy(env[l][:], env_win[:].indirect(lists[l][:]))

        def gather_words(l, g):
            whole = sbuf([P, S], U32, "xw%d%d" % (l, g))
            nc.vector.tensor_copy(whole[:], word_win[g][:].bitcast(U32).indirect(lists[l][:]))
            xw[l, g, 0] = whole[:, 0:HALF]
            xw[l, g, 1] = whole[:, HALF:S]

        def gather_half(l, g, h):
            if (l, h) == (1, 1):
                half = sbuf([P, HALF], U32, "xw_last")[:]
            else:
                if g not in held:
                    held[g] = sbuf([P, 3 * HALF], U32, "xw%d" % g)
                half = held[g][:, l * S + h * HALF:l * S + (h + 1) * HALF]
            nc.vector.tensor_copy(half, word_win[g][:].bitcast(U32).indirect(lists[l][:, 16 * h:16 * (h + 1)]))
            xw[l, g, h] = half

        recip = keep.tile([P, JT + 2 * MT], F32, name="recip")
        scaled = keep.tile([P, JT, 2], F32, name="scaled")
        lag_gain = keep.tile([P, JT], F32, name="lag_gain")
        gains = [lambda t: recip[:, t:t + 1], lambda t: scaled[:, t, 0:1], lambda t: lag_gain[:, t:t + 1]]

        def load_env():
            nc.sync.dma_start(env_win[0:1, :], envl[0:1, :])

        def small():
            held["pair"] = sbuf([P, 2 * JT + JT + MT], F32, "pair")
            positive = held["pair"][:, 2 * JT:3 * JT + MT]
            held["floored"] = floored = sbuf([P, JT + 2 * MT], F32, "floored")
            nc.scalar.activation(positive[:, 0:JT], held["one_ps"][:, 0:JT], ACT.Relu)
            nc.scalar.activation(positive[:, JT:JT + MT], held["inv_t"][:], ACT.Relu)
            nc.scalar.activation(floored[:, 0:JT + MT], positive, ACT.Copy, bias=FLOOR)
            nc.scalar.activation(floored[:, JT + MT:JT + 2 * MT], positive[:, JT:JT + MT], ACT.Copy, scale=-1.0, bias=-FLOOR)

        def small2():
            nc.vector.reciprocal(recip[:], held["floored"][:])

        def load_inv():
            held["inv_t"] = inv_t = sbuf([P, MT], F32, "inv_t")
            with nc.allow_non_contiguous_dma(reason="one value a partition"):
                nc.sync.dma_start(inv_t[:], inv.rearrange("(t p) o -> p (t o)", p=P))

        def make_gains():
            env_ps = []
            pair = held["pair"][:, 0:2 * JT].rearrange("p (t e) -> p t e", e=2)
            for l in range(2):
                env_ps.append(psum.tile([P, JT, P], F32, name="env_ps%d" % l, tag="out_%d" % l))
                for t in range(JT):
                    nc.tensor.transpose(env_ps[l][:, t, :], env[l][:, t * P:(t + 1) * P], ident[:])
            nc.scalar.activation(pair[:, :, 0], env_ps[0][:, :, 96], ACT.Square)
            nc.scalar.activation(pair[:, :, 1], env_ps[1][:, :, 96], ACT.Copy)
            for t in range(JT):
                nc.scalar.activation(scaled[:, t, :], pair[:, t, :], ACT.Copy, scale=recip[:, t:t + 1])
            for t in range(JT):
                nc.scalar.activation(lag_gain[:, t:t + 1], scaled[:, t, 0:1], ACT.Identity, scale=0.5, bias=scaled[:, t, 1:2])

        def product(i, g, h):
            l = 0 if i < 2 else 1
            if g == 0:
                banks[i, h] = psum.tile([P, 2, N], F32, name="y%d_%d" % (i, h), tag="y%d_%d" % (i, h))
            for u in range(2):
                nc.tensor.matmul_mx(
                    out=banks[i, h][:, u, :],
                    lhsT=xw[l, g, h][:, u * P:(u + 1) * P].bitcast(FP8X4),
                    lhsT_scale=xs[l][4 * g:P, (2 * h + u) * P:(2 * h + u + 1) * P],
                    rhs=codes[i, g][:].bitcast(FP8X4),
                    rhs_scale=planes[i, g][:],
                    start=(g == 0 and u == 0),
                    stop=(g == PASSES - 1 and u == 1),
                )

        def weigh(i, h, eng, onto=None):
            for u in range(2):
                t = 2 * h + u
                if t == 0:
                    held["term", i] = sbuf([P, JT, N], F32, "term%d" % i)
                terms[i, t] = held["term", i][:, t, :]
                src = banks[i, h][:, u, :]
                if eng == "s":
                    nc.scalar.activation(terms[i, t], src, ACT.Copy, scale=gains[i](t))
                elif onto is None:
                    nc.vector.tensor_scalar(terms[i, t], src, gains[i](t), None, ALU.mult)
                else:
                    nc.vector.scalar_tensor_tensor(terms[i, t], src, gains[i](t), terms[onto, t], ALU.mult, ALU.add)

        def turn(i, h):
            if i == 0:
                sums[h] = psum.tile([P, MT, HALF], F32, name="sum%d" % h, tag="out_%d" % h)
            for u in range(2):
                for mt in range(MT):
                    nc.tensor.matmul(
                        sums[h][:, mt, u * P:(u + 1) * P],
                        terms[i, 2 * h + u][:, mt * P:(mt + 1) * P],
                        ident[:],
                        start=(i == 0 and u == 0 and mt == 0),
                        stop=(i == 2 and u == 1 and mt == MT - 1),
                        is_transpose=True,
                    )

        def finish(h):
            res = sbuf([P, MT, HALF], F32, "res%d" % h)
            for mt in range(MT):
                nc.vector.tensor_scalar(res[:, mt, :], sums[h][:, mt, :], recip[:, JT + mt:JT + mt + 1], recip[:, JT + MT + mt:JT + MT + mt + 1], ALU.min, ALU.max)
                (nc.sync if mt else nc.scalar).dma_start(out[mt * P:(mt + 1) * P, h * HALF:(h + 1) * HALF], res[:, mt, :])

        load_w(0, 0)
        load_w(1, 0)
        load_w(2, 0)
        load_one()
        load_inv()
        load_x(0)
        load_w(0, 1)
        gather_scales(0)
        gather_scales(1)
        gather_env(0)
        gather_env(1)
        cast_w(0, 0, "a")
        cast_w(1, 0, "s")
        cast_w(2, 0, "s")
        load_x(1)
        small()
        quant_w(0, 0)
        small2()
        make_gains()
        load_w(1, 1)
        quant_w(1, 0)
        quant_w(2, 0)
        load_w(2, 1)
        gather_words(0, 0)
        gather_words(1, 0)
        for i in range(3):
            product(i, 0, 0)
            product(i, 0, 1)
        cast_w(0, 1, "s")
        quant_w(0, 1)
        gather_half(0, 1, 0)
        gather_half(0, 1, 1)
        product(0, 1, 0)
        product(0, 1, 1)
        gather_half(1, 1, 0)
        cast_w(1, 1, "s")
        quant_w(1, 1)
        product(1, 1, 0)
        product(1, 1, 1)
        cast_w(2, 1, "v")
        quant_w(2, 1)
        gather_half(1, 1, 1)
        weigh(0, 0, "s")
        weigh(0, 1, "s")
        weigh(1, 0, "s")
        weigh(1, 1, "s")
        product(2, 1, 0)
        product(2, 1, 1)
        turn(0, 0)
        turn(0, 1)
        weigh(2, 0, "v", 1)
        turn(1, 1)
        weigh(2, 1, "s")
        turn(2, 0)
        turn(2, 1)
        finish(0)
        finish(1)
